import numpy as np
import ml_dtypes


def mxq(x, axis, fmt="e4m3"):
    dtype, down = {"e4m3": (ml_dtypes.float8_e4m3fn, 7), "e5m2": (ml_dtypes.float8_e5m2, 14)}[fmt]
    v = np.moveaxis(np.asarray(x, np.float32).astype(ml_dtypes.bfloat16).astype(np.float64), axis, -1)
    blocks = v.reshape(v.shape[:-1] + (-1, 32))
    amax = np.abs(blocks).max(-1, keepdims=True)
    byte = np.maximum(np.where(amax > 0, np.frexp(amax)[1] - 1 + 127, 0) - down, 1)
    scale = np.exp2(byte - 127.0)
    codes = (blocks / scale).astype(np.float32).astype(dtype).astype(np.float64)
    return np.moveaxis((codes * scale).reshape(v.shape), -1, axis)


WIDE = False


def mx_kscale(k):
    if not WIDE:
        return np.ones(k)
    levels = np.array([10, -10, 5, -5, 0])
    if k % 512:
        return np.exp2(np.random.permutation(np.resize(levels, k // 32))).repeat(32)
    a = np.empty((k // 512, 16))
    for p in range(k // 512):
        a[p, :8] = np.random.permutation(np.resize(levels, 8))
        for g in range(8):
            far = levels[np.abs(levels - a[p, g]) >= 10]
            a[p, g + 8] = far[np.random.randint(len(far))]
    return np.exp2(a.ravel()).repeat(32)


def f64(x):
    return np.asarray(x).astype(np.float64)


def striped(idx):
    return np.tile(np.asarray(idx).reshape(-1, 16).T, (8, 1)).astype(np.uint16)


def unstriped(offs):
    return offs[:16].T.reshape(-1).astype(np.int64)


E2M1 = np.array([0.0, 0.5, 1.0, 1.5, 2.0, 3.0, 4.0, 6.0, -0.0, -0.5, -1.0, -1.5, -2.0, -3.0, -4.0, -6.0])


def pack_weight(w, fmt):
    k, n = w.shape
    w = f64(np.asarray(w, np.float32).astype(ml_dtypes.bfloat16)).reshape(k // 32, 32, n)
    amax = np.abs(w).max(1)
    if fmt == "e4m3":
        byte = np.frexp(amax)[1] - 1 + 127 - 7
    else:
        mant, ex = np.frexp(amax / 6.0)
        byte = np.where(mant > 0.5, ex, ex - 1) + 127
    byte = np.clip(np.where(amax > 0, byte, 1), 1, 254)
    scaled = (w * np.exp2(127.0 - byte)[:, None, :]).reshape(k, n).astype(np.float32)
    by_word = np.ascontiguousarray(scaled.reshape(k // 512, 128, 4, n).transpose(0, 1, 3, 2))
    if fmt == "e4m3":
        words = by_word.astype(ml_dtypes.float8_e4m3fn).view(np.uint8)
    else:
        c = by_word.astype(ml_dtypes.float4_e2m1fn).view(np.uint8) & 0xF
        words = (c[..., 0::2] | (c[..., 1::2] << 4)).reshape(k // 512, 128, 2 * n)
    return np.ascontiguousarray(words), np.ascontiguousarray(byte.astype(np.uint8).reshape(k // 512, 16, n))


def unpack_weight(words, scales, fmt):
    g, _, n = scales.shape
    words = np.ascontiguousarray(words).reshape(g, 128, n, -1)
    if fmt == "e4m3":
        vals = words.view(ml_dtypes.float8_e4m3fn).astype(np.float64)
    else:
        nib = np.empty((g, 128, n, 4), np.uint8)
        nib[..., 0::2] = words & 0xF
        nib[..., 1::2] = words >> 4
        vals = E2M1[nib]
    vals = vals * np.repeat(np.exp2(scales.astype(np.float64) - 127.0), 8, axis=1)[..., None]
    return vals.transpose(0, 1, 3, 2).reshape(g * 512, n)


D, T, I, Q, E, Z, X = 512, 2048, 512, 128, 512, 1024, 1024


def setup_inputs():
    n = np.random.standard_normal
    idx = np.random.permutation(T)[:I]
    idx2 = np.random.permutation(Z)[:I]
    idx3 = np.random.permutation(Z)[:I]
    idx4 = np.random.permutation(X)[:I]
    fd = mx_kscale(D)
    fi = mx_kscale(I)
    keysp = pack_weight(n((D, T)) / fd[:, None], "e4m3")
    return {
        "query": (n((D, Q)) * 1.0 / np.sqrt(D) * fd[:, None]).astype(np.float32),
        "keys_words": keysp[0],
        "keys_scales": keysp[1],
        "os": (np.random.uniform(0.02, 0.08, (1, I)) * fi).astype(np.float32),
        "vals": (n((E, T))).astype(np.float32),
        "vals2": (n((E, X))).astype(np.float32),
        "vsc": (np.random.uniform(0.5, 2.0, (1, I)) / fi).astype(np.float32),
        "offs": striped(idx),
        "offs2": striped(idx2),
        "offs3": striped(idx3),
        "offs4": striped(idx4),
    }


def reference(query, keys_words, keys_scales, os, vals, vals2, vsc, offs, offs2, offs3, offs4):
    idx = unstriped(offs)
    idx2 = unstriped(offs2)
    idx3 = unstriped(offs3)
    idx4 = unstriped(offs4)
    keysu = unpack_weight(keys_words, keys_scales, "e4m3")
    queryq = mxq(f64(query), 0, "e4m3")
    keysidxg = keysu[:, idx]
    a = queryq.T @ keysidxg
    f0 = np.zeros((Q, Z))
    f0[:, idx2] = a
    w = a + f0[:, idx3]
    wo1 = w * f64(os)
    wt1 = wo1.T
    vz = np.abs(f64(vals)[:, idx] - f64(vals2)[:, idx4]) * f64(vsc)
    vt1 = vz.T
    wt1q = mxq(wt1, 0, "e4m3")
    vt1q = mxq(vt1, 0, "e4m3")
    o = wt1q.T @ vt1q
    return o

@@ -1,0 +1,186 @@
+from contextlib import ExitStack
+
+import concourse.mybir as mybir
+from concourse.masks import make_identity
+
+D, T, I, Q, E, Z, X = 512, 2048, 512, 128, 512, 1024, 1024
+FLOPS = 2 * Q * D * I + 2 * Q * I * E
+
+F32 = mybir.dt.float32
+BF16 = mybir.dt.bfloat16
+I32 = mybir.dt.int32
+U32 = mybir.dt.uint32
+U16 = mybir.dt.uint16
+U8 = mybir.dt.uint8
+FP8X4 = mybir.dt.float8_e4m3fn_x4
+COPY = mybir.ActivationFunctionType.Copy
+ABS = mybir.ActivationFunctionType.Abs
+MULT = mybir.AluOpType.mult
+
+P = 128
+PACK = 4
+BLOCKS = E // P
+LIST_COLS = I // 16
+
+
+def tile_attend_passedthrough_apartvalues_lean_kernel(
+    tc, query, keys_words, keys_scales, weight_factor, vals, vals2, value_factor, offs, offs2, offs3, offs4, out
+):
+    nc = tc.nc
+    with ExitStack() as ctx:
+        sb = ctx.enter_context(tc.tile_pool(name="sb", bufs=1))
+        ps = ctx.enter_context(tc.psum_pool(name="ps", bufs=1))
+
+        def load_list(name, src):
+            tile = sb.tile([P, LIST_COLS], U16, name=name)
+            nc.sync.dma_start(tile[:], src)
+            return tile
+
+        def load_columns(name, src):
+            tile = sb.tile([P, PACK], F32, name=name)
+            nc.sync.dma_start(tile[:], src.rearrange("o (p t) -> (o p) t", t=PACK))
+            return tile
+
+        def load_rows(name, src, b):
+            tile = sb.tile([P, src.shape[1]], F32, name=name, tag=name, align_bytes=64)
+            nc.sync.dma_start(tile[:], src[b * P : (b + 1) * P, :])
+            return tile
+
+        def turn(bank, columns, start, stop):
+            for t in range(PACK):
+                nc.tensor.matmul(
+                    bank[:, t, :], columns(t), identity[:], is_transpose=True,
+                    start=start and t == 0, stop=stop and t == PACK - 1,
+                )
+
+        def quantise(name, grouped, width):
+            codes = sb.tile([P, width], U32, name=name + "_codes", align_bytes=64)
+            scales = sb.tile([P, width], U8, name=name + "_scales", align_bytes=64)
+            nc.vector.quantize_mx(
+                out=codes[:].bitcast(FP8X4), scales=scales[:], in_=grouped[:].rearrange("p c t -> p (c t)")
+            )
+            return codes, scales
+
+        first = [None] * BLOCKS
+        second = [None] * BLOCKS
+        store_list = load_list("store_list", offs4)
+        second[0] = load_rows("second0", vals2, 0)
+        token_list = load_list("token_list", offs)
+        key_scale_pool = sb.tile([P, T], U8, name="key_scale_pool")
+        for quadrant in (0, 2, 1, 3):
+            rows = keys_scales[0, PACK * quadrant : PACK * (quadrant + 1), :].bitcast(I32)
+            nc.sync.dma_start(
+                key_scale_pool[32 * quadrant : 32 * (quadrant + 1), :].bitcast(I32),
+                rows.unsqueeze(0).to_broadcast([8, PACK, T // 4]),
+            )
+        query_raw = sb.tile([P, PACK, Q], F32, name="query_raw")
+        nc.sync.dma_start(query_raw[:], query.rearrange("(p t) q -> p t q", t=PACK))
+        key_word_pool = sb.tile([P, T], U32, name="key_word_pool")
+        nc.sync.dma_start(
+            key_word_pool[:].bitcast(I32), keys_words[0].rearrange("p n t -> p (n t)").bitcast(I32)
+        )
+        first[0] = load_rows("first0", vals, 0)
+        put_list = load_list("put_list", offs2)
+        second[1] = load_rows("second1", vals2, 1)
+        fetch_list = load_list("fetch_list", offs3)
+        value_cols = load_columns("value_cols", value_factor)
+        weight_cols = load_columns("weight_cols", weight_factor)
+        first[1] = load_rows("first1", vals, 1)
+        for b in range(2, BLOCKS):
+            second[b] = load_rows("second%d" % b, vals2, b)
+            first[b] = load_rows("first%d" % b, vals, b)
+
+        identity = sb.tile([P, P], F32, name="identity")
+        make_identity(nc, identity[:])
+        places = sb.tile([P, Z], F32, name="places")
+        nc.gpsimd.memset(places[:], 0.0)
+
+        def gather_on_scalar(name, window, offsets, scale, tag):
+            picked = sb.tile([P, I], F32, name=name, tag=tag, align_bytes=64)
+            nc.scalar.activation(picked[:], window[:].indirect(offsets[:]), COPY, scale=scale)
+            return lambda t: picked[:, t:I:PACK]
+
+        def gather_on_vector(name, window, offsets):
+            dealt = sb.tile([P, PACK, P], F32, name=name)
+            nc.vector.tensor_copy(dealt[:].rearrange("p t s -> p s t"), window[:].indirect(offsets[:]))
+            return lambda t: dealt[:, t, :]
+
+        def open_block(b):
+            name = "minus_second%d" % b
+            bank = ps.tile([P, PACK, P], F32, name="value_bank%d" % b, tag="value_bank%d" % b)
+            turn(bank, gather_on_scalar(name, second[b], store_list, -1.0, name), True, False)
+            return bank
+
+        def absolute(b, tag):
+            apart = sb.tile([P, P, PACK], F32, name="apart%d" % b, tag=tag, align_bytes=64)
+            nc.scalar.activation(apart[:], banks[b][:].rearrange("p t e -> p e t"), ABS)
+            return apart[:]
+
+        def times(grouped, values, cols):
+            nc.vector.tensor_tensor(grouped, values, cols[:].unsqueeze(1).to_broadcast([P, P, PACK]), MULT)
+
+        def finish(b0, operands, tag):
+            width = len(operands) * P
+            bank = ps.tile([P, width], F32, name="out_bank%d" % b0, tag=tag)
+            for j, (codes, scales) in enumerate(operands):
+                nc.tensor.matmul_mx(
+                    out=bank[:, j * P : (j + 1) * P], lhsT=weight_codes.bitcast(FP8X4), lhsT_scale=weight_scales,
+                    rhs=codes.bitcast(FP8X4), rhs_scale=scales, start=True, stop=True,
+                )
+            result = sb.tile([P, width], F32, name="result%d" % b0)
+            nc.scalar.copy(result[:], bank[:])
+            nc.sync.dma_start(out[:, b0 * P : b0 * P + width], result[:])
+
+        banks = [open_block(0)]
+
+        key_scales = sb.tile([P, I], U8, name="key_scales", align_bytes=64)
+        nc.vector.tensor_copy(key_scales[:], key_scale_pool[:].indirect(token_list[:]))
+        query_grouped = sb.tile([P, Q, PACK], BF16, name="query_grouped", align_bytes=64)
+        nc.vector.tensor_copy(query_grouped[:], query_raw[:].rearrange("p t q -> p q t"))
+        query_codes, query_scales = quantise("query", query_grouped, Q)
+        key_words = sb.tile([P, I], U32, name="key_words", align_bytes=64)
+        nc.vector.tensor_copy(key_words[:], key_word_pool[:].indirect(token_list[:]))
+
+        score_bank = ps.tile([P, I], F32, name="score_bank")
+        nc.tensor.matmul_mx(
+            out=score_bank[:], lhsT=query_codes[:].bitcast(FP8X4), lhsT_scale=query_scales[:],
+            rhs=key_words[:].bitcast(FP8X4), rhs_scale=key_scales[:], start=True, stop=True,
+        )
+        scores = sb.tile([P, I], F32, name="scores")
+        nc.vector.tensor_copy(scores[:], score_bank[:])
+        nc.vector.tensor_copy(places[:].indirect(put_list[:]), scores[:])
+        weight_bank = ps.tile([P, PACK, Q], F32, name="weight_bank")
+        turn(weight_bank, lambda t: scores[:, t:I:PACK], True, False)
+
+        turn(banks[0], gather_on_scalar("first_picked0", first[0], token_list, 1.0, "first_picked0"), False, True)
+        banks.append(open_block(1))
+        apart0 = absolute(0, "apart0")
+        turn(weight_bank, gather_on_scalar("fetched", places, fetch_list, 1.0, "second1"), False, True)
+
+        turn(banks[1], gather_on_vector("first_dealt1", first[1], token_list), False, True)
+        grouped0 = sb.tile([P, P, PACK], BF16, name="grouped0", tag="first1", align_bytes=64)
+        times(grouped0[:], apart0, value_cols)
+        codes0, scales0 = quantise("value0", grouped0, P)
+        banks.append(open_block(2))
+        apart1 = absolute(1, "apart1")
+
+        turn(banks[2], gather_on_vector("first_dealt2", first[2], token_list), False, True)
+        grouped1 = sb.tile([P, Q + P, PACK], BF16, name="grouped1", tag="first2", align_bytes=64)
+        times(grouped1[:, :Q, :], weight_bank[:].rearrange("p t q -> p q t"), weight_cols)
+        times(grouped1[:, Q:, :], apart1, value_cols)
+        codes1, scales1 = quantise("value1", grouped1, Q + P)
+        weight_codes, weight_scales = codes1[:, :Q], scales1[:, :Q]
+        banks.append(open_block(3))
+        apart2 = absolute(2, "second3")
+
+        turn(banks[3], gather_on_vector("first_dealt3", first[3], token_list), False, True)
+        finish(0, [(codes0[:], scales0[:]), (codes1[:, Q:], scales1[:, Q:])], "value_bank2")
+        grouped2 = sb.tile([P, P, PACK], BF16, name="grouped2", tag="first3", align_bytes=64)
+        times(grouped2[:], apart2, value_cols)
+        apart3 = absolute(3, "apart3")
+        codes2, scales2 = quantise("value2", grouped2, P)
+        grouped3 = sb.tile([P, P, PACK], BF16, name="grouped3", align_bytes=64)
+        times(grouped3[:], apart3, value_cols)
+        codes3, scales3 = quantise("value3", grouped3, P)
+        finish(2, [(codes2[:], scales2[:])], "out2")
+        finish(3, [(codes3[:], scales3[:])], "out3")

@@ -57,14 +57,12 @@ def tile_attend_passedthrough_apartvalues_lean_kernel(
             codes = sb.tile([P, width], U32, name=name + "_codes", align_bytes=64)
             scales = sb.tile([P, width], U8, name=name + "_scales", align_bytes=64)
             nc.vector.quantize_mx(
-                out=codes[:].bitcast(FP8X4), scales=scales[:], in_=grouped[:].rearrange("p c t -> p (c t)")
+                out=codes[:].bitcast(FP8X4), scales=scales[:], in_=grouped
             )
             return codes, scales
 
         first = [None] * BLOCKS
         second = [None] * BLOCKS
-        store_list = load_list("store_list", offs4)
-        second[0] = load_rows("second0", vals2, 0)
         token_list = load_list("token_list", offs)
         key_scale_pool = sb.tile([P, T], U8, name="key_scale_pool")
         for quadrant in (0, 2, 1, 3):
@@ -79,6 +77,8 @@ def tile_attend_passedthrough_apartvalues_lean_kernel(
         nc.sync.dma_start(
             key_word_pool[:].bitcast(I32), keys_words[0].rearrange("p n t -> p (n t)").bitcast(I32)
         )
+        store_list = load_list("store_list", offs4)
+        second[0] = load_rows("second0", vals2, 0)
         first[0] = load_rows("first0", vals, 0)
         put_list = load_list("put_list", offs2)
         second[1] = load_rows("second1", vals2, 1)
@@ -95,9 +95,8 @@ def tile_attend_passedthrough_apartvalues_lean_kernel(
         places = sb.tile([P, Z], F32, name="places")
         nc.gpsimd.memset(places[:], 0.0)
 
-        def gather_on_scalar(name, window, offsets, scale, tag):
-            picked = sb.tile([P, I], F32, name=name, tag=tag, align_bytes=64)
-            nc.scalar.activation(picked[:], window[:].indirect(offsets[:]), COPY, scale=scale)
+        def gather_on_scalar(picked, window, offsets, scale):
+            nc.scalar.activation(picked, window[:].indirect(offsets[:]), COPY, scale=scale)
             return lambda t: picked[:, t:I:PACK]
 
         def gather_on_vector(name, window, offsets):
@@ -105,10 +104,9 @@ def tile_attend_passedthrough_apartvalues_lean_kernel(
             nc.vector.tensor_copy(dealt[:].rearrange("p t s -> p s t"), window[:].indirect(offsets[:]))
             return lambda t: dealt[:, t, :]
 
-        def open_block(b):
-            name = "minus_second%d" % b
+        def open_block(b, picked):
             bank = ps.tile([P, PACK, P], F32, name="value_bank%d" % b, tag="value_bank%d" % b)
-            turn(bank, gather_on_scalar(name, second[b], store_list, -1.0, name), True, False)
+            turn(bank, gather_on_scalar(picked, second[b], store_list, -1.0), True, False)
             return bank
 
         def absolute(b, tag):
@@ -117,9 +115,16 @@ def tile_attend_passedthrough_apartvalues_lean_kernel(
             return apart[:]
 
         def times(grouped, values, cols):
-            nc.vector.tensor_tensor(grouped, values, cols[:].unsqueeze(1).to_broadcast([P, P, PACK]), MULT)
+            nc.vector.tensor_tensor(
+                grouped.rearrange("p (c t) -> p c t", t=PACK), values,
+                cols[:].unsqueeze(1).to_broadcast([P, values.shape[1], PACK]), MULT,
+            )
 
-        def finish(b0, operands, tag):
+        def over_first(b):
+            tenant = sb.tile([P, 2 * I], F32, name="over_first%d" % b, tag="first%d" % b, align_bytes=64)
+            return tenant[:, :I], tenant[:, I:].bitcast(BF16)
+
+        def finish(b0, operands, tag, queue):
             width = len(operands) * P
             bank = ps.tile([P, width], F32, name="out_bank%d" % b0, tag=tag)
             for j, (codes, scales) in enumerate(operands):
@@ -129,15 +134,13 @@ def tile_attend_passedthrough_apartvalues_lean_kernel(
                 )
             result = sb.tile([P, width], F32, name="result%d" % b0)
             nc.scalar.copy(result[:], bank[:])
-            nc.sync.dma_start(out[:, b0 * P : b0 * P + width], result[:])
-
-        banks = [open_block(0)]
+            queue.dma_start(out[:, b0 * P : b0 * P + width], result[:])
 
         key_scales = sb.tile([P, I], U8, name="key_scales", align_bytes=64)
         nc.vector.tensor_copy(key_scales[:], key_scale_pool[:].indirect(token_list[:]))
         query_grouped = sb.tile([P, Q, PACK], BF16, name="query_grouped", align_bytes=64)
-        nc.vector.tensor_copy(query_grouped[:], query_raw[:].rearrange("p t q -> p q t"))
-        query_codes, query_scales = quantise("query", query_grouped, Q)
+        nc.scalar.copy(query_grouped[:], query_raw[:].rearrange("p t q -> p q t"))
+        query_codes, query_scales = quantise("query", query_grouped[:].rearrange("p c t -> p (c t)"), Q)
         key_words = sb.tile([P, I], U32, name="key_words", align_bytes=64)
         nc.vector.tensor_copy(key_words[:], key_word_pool[:].indirect(token_list[:]))
 
@@ -149,38 +152,48 @@ def tile_attend_passedthrough_apartvalues_lean_kernel(
         scores = sb.tile([P, I], F32, name="scores")
         nc.vector.tensor_copy(scores[:], score_bank[:])
         nc.vector.tensor_copy(places[:].indirect(put_list[:]), scores[:])
+
+        minus_second0 = sb.tile([P, I], F32, name="minus_second0")
+        banks = [open_block(0, minus_second0[:])]
         weight_bank = ps.tile([P, PACK, Q], F32, name="weight_bank")
         turn(weight_bank, lambda t: scores[:, t:I:PACK], True, False)
 
-        turn(banks[0], gather_on_scalar("first_picked0", first[0], token_list, 1.0, "first_picked0"), False, True)
-        banks.append(open_block(1))
-        apart0 = absolute(0, "apart0")
-        turn(weight_bank, gather_on_scalar("fetched", places, fetch_list, 1.0, "second1"), False, True)
+        first_picked0 = sb.tile([P, I], F32, name="first_picked0", tag="picked")
+        turn(banks[0], gather_on_scalar(first_picked0[:], first[0], token_list, 1.0), False, True)
+        minus_second1 = sb.tile([P, I], F32, name="minus_second1")
+        banks.append(open_block(1, minus_second1[:]))
+        apart0 = absolute(0, "second1")
+        fetched = sb.tile([P, I], F32, name="fetched", tag="picked")
+        turn(weight_bank, gather_on_scalar(fetched[:], places, fetch_list, 1.0), False, True)
 
         turn(banks[1], gather_on_vector("first_dealt1", first[1], token_list), False, True)
-        grouped0 = sb.tile([P, P, PACK], BF16, name="grouped0", tag="first1", align_bytes=64)
-        times(grouped0[:], apart0, value_cols)
-        codes0, scales0 = quantise("value0", grouped0, P)
-        banks.append(open_block(2))
-        apart1 = absolute(1, "apart1")
+        minus_second2, grouped0 = over_first(1)
+        times(grouped0[:, I:], apart0, value_cols)
+        times(grouped0[:, :I], weight_bank[:].rearrange("p t q -> p q t"), weight_cols)
+        codes0, scales0 = quantise("value0", grouped0, Q + P)
+        weight_codes, weight_scales = codes0[:, :Q], scales0[:, :Q]
+        banks.append(open_block(2, minus_second2))
+        apart1 = absolute(1, "second2")
 
         turn(banks[2], gather_on_vector("first_dealt2", first[2], token_list), False, True)
-        grouped1 = sb.tile([P, Q + P, PACK], BF16, name="grouped1", tag="first2", align_bytes=64)
-        times(grouped1[:, :Q, :], weight_bank[:].rearrange("p t q -> p q t"), weight_cols)
-        times(grouped1[:, Q:, :], apart1, value_cols)
-        codes1, scales1 = quantise("value1", grouped1, Q + P)
-        weight_codes, weight_scales = codes1[:, :Q], scales1[:, :Q]
-        banks.append(open_block(3))
+        minus_second3, grouped1 = over_first(2)
+        times(grouped1[:, :I], apart1, value_cols)
+        codes1, scales1 = quantise("value1", grouped1[:, :I], P)
+        banks.append(open_block(3, minus_second3))
         apart2 = absolute(2, "second3")
 
         turn(banks[3], gather_on_vector("first_dealt3", first[3], token_list), False, True)
-        finish(0, [(codes0[:], scales0[:]), (codes1[:, Q:], scales1[:, Q:])], "value_bank2")
-        grouped2 = sb.tile([P, P, PACK], BF16, name="grouped2", tag="first3", align_bytes=64)
+        finish(0, [(codes0[:, Q:], scales0[:, Q:]), (codes1[:], scales1[:])], "value_bank2", nc.sync)
+        grouped2 = sb.tile([P, I], BF16, name="grouped2", tag="first3", align_bytes=64)
         times(grouped2[:], apart2, value_cols)
-        apart3 = absolute(3, "apart3")
-        codes2, scales2 = quantise("value2", grouped2, P)
-        grouped3 = sb.tile([P, P, PACK], BF16, name="grouped3", align_bytes=64)
-        times(grouped3[:], apart3, value_cols)
-        codes3, scales3 = quantise("value3", grouped3, P)
-        finish(2, [(codes2[:], scales2[:])], "out2")
-        finish(3, [(codes3[:], scales3[:])], "out3")
+        apart3 = sb.tile([P, P, PACK], F32, name="apart3")
+        for h in range(2):
+            columns = slice(h * P // 2, (h + 1) * P // 2)
+            nc.scalar.activation(apart3[:, columns, :], banks[3][:, :, columns].rearrange("p t e -> p e t"), ABS)
+        codes2, scales2 = quantise("value2", grouped2[:], P)
+        grouped3 = sb.tile([P, I], BF16, name="grouped3", align_bytes=64)
+        for h in range(2):
+            times(grouped3[:, h * I // 2 : (h + 1) * I // 2], apart3[:, h * P // 2 : (h + 1) * P // 2, :], value_cols)
+        codes3, scales3 = quantise("value3", grouped3[:], P)
+        finish(2, [(codes2[:], scales2[:])], "out2", nc.sync)
+        finish(3, [(codes3[:], scales3[:])], "out3", nc.scalar)

@@ -63,16 +63,13 @@ def tile_attend_passedthrough_apartvalues_lean_kernel(
 
         first = [None] * BLOCKS
         second = [None] * BLOCKS
-        token_list = load_list("token_list", offs)
         key_scale_pool = sb.tile([P, T], U8, name="key_scale_pool")
-        for quadrant in (0, 2, 1, 3):
-            rows = keys_scales[0, PACK * quadrant : PACK * (quadrant + 1), :].bitcast(I32)
-            nc.sync.dma_start(
-                key_scale_pool[32 * quadrant : 32 * (quadrant + 1), :].bitcast(I32),
-                rows.unsqueeze(0).to_broadcast([8, PACK, T // 4]),
-            )
+        nc.gpsimd.memset(key_scale_pool[:].bitcast(I32), 0)
         query_raw = sb.tile([P, PACK, Q], F32, name="query_raw")
         nc.sync.dma_start(query_raw[:], query.rearrange("(p t) q -> p t q", t=PACK))
+        token_list = load_list("token_list", offs)
+        for f in range(PACK):
+            nc.sync.dma_start(key_scale_pool[f:P:32, :].bitcast(I32), keys_scales[0, f:16:PACK, :].bitcast(I32))
         key_word_pool = sb.tile([P, T], U32, name="key_word_pool")
         nc.sync.dma_start(
             key_word_pool[:].bitcast(I32), keys_words[0].rearrange("p n t -> p (n t)").bitcast(I32)
@@ -141,16 +138,20 @@ def tile_attend_passedthrough_apartvalues_lean_kernel(
         query_grouped = sb.tile([P, Q, PACK], BF16, name="query_grouped", align_bytes=64)
         nc.scalar.copy(query_grouped[:], query_raw[:].rearrange("p t q -> p q t"))
         query_codes, query_scales = quantise("query", query_grouped[:].rearrange("p c t -> p (c t)"), Q)
-        key_words = sb.tile([P, I], U32, name="key_words", align_bytes=64)
-        nc.vector.tensor_copy(key_words[:], key_word_pool[:].indirect(token_list[:]))
-
-        score_bank = ps.tile([P, I], F32, name="score_bank")
-        nc.tensor.matmul_mx(
-            out=score_bank[:], lhsT=query_codes[:].bitcast(FP8X4), lhsT_scale=query_scales[:],
-            rhs=key_words[:].bitcast(FP8X4), rhs_scale=key_scales[:], start=True, stop=True,
-        )
         scores = sb.tile([P, I], F32, name="scores")
-        nc.vector.tensor_copy(scores[:], score_bank[:])
+        half = I // 2
+        key_words = [sb.tile([P, half], U32, name="key_words%d" % h, align_bytes=64) for h in range(2)]
+        score_banks = [ps.tile([P, half], F32, name="score_bank%d" % h, tag="score_bank%d" % h) for h in range(2)]
+        for h in range(2):
+            entries = token_list[:, h * half // 16 : (h + 1) * half // 16]
+            nc.vector.tensor_copy(key_words[h][:], key_word_pool[:].indirect(entries))
+            nc.tensor.matmul_mx(
+                out=score_banks[h][:], lhsT=query_codes[:].bitcast(FP8X4), lhsT_scale=query_scales[:],
+                rhs=key_words[h][:].bitcast(FP8X4), rhs_scale=key_scales[:, h * half : (h + 1) * half],
+                start=True, stop=True,
+            )
+        for h in range(2):
+            nc.vector.tensor_copy(scores[:, h * half : (h + 1) * half], score_banks[h][:])
         nc.vector.tensor_copy(places[:].indirect(put_list[:]), scores[:])
 
         minus_second0 = sb.tile([P, I], F32, name="minus_second0")
@@ -168,22 +169,22 @@ def tile_attend_passedthrough_apartvalues_lean_kernel(
 
         turn(banks[1], gather_on_vector("first_dealt1", first[1], token_list), False, True)
         minus_second2, grouped0 = over_first(1)
-        times(grouped0[:, I:], apart0, value_cols)
-        times(grouped0[:, :I], weight_bank[:].rearrange("p t q -> p q t"), weight_cols)
-        codes0, scales0 = quantise("value0", grouped0, Q + P)
-        weight_codes, weight_scales = codes0[:, :Q], scales0[:, :Q]
+        times(grouped0[:, :I], apart0, value_cols)
+        codes0, scales0 = quantise("value0", grouped0[:, :I], P)
         banks.append(open_block(2, minus_second2))
         apart1 = absolute(1, "second2")
 
         turn(banks[2], gather_on_vector("first_dealt2", first[2], token_list), False, True)
         minus_second3, grouped1 = over_first(2)
-        times(grouped1[:, :I], apart1, value_cols)
-        codes1, scales1 = quantise("value1", grouped1[:, :I], P)
+        times(grouped1[:, :I], weight_bank[:].rearrange("p t q -> p q t"), weight_cols)
+        times(grouped1[:, I:], apart1, value_cols)
+        codes1, scales1 = quantise("value1", grouped1, Q + P)
+        weight_codes, weight_scales = codes1[:, :Q], scales1[:, :Q]
         banks.append(open_block(3, minus_second3))
         apart2 = absolute(2, "second3")
 
         turn(banks[3], gather_on_vector("first_dealt3", first[3], token_list), False, True)
-        finish(0, [(codes0[:, Q:], scales0[:, Q:]), (codes1[:], scales1[:])], "value_bank2", nc.sync)
+        finish(0, [(codes0[:], scales0[:]), (codes1[:, Q:], scales1[:, Q:])], "value_bank2", nc.sync)
         grouped2 = sb.tile([P, I], BF16, name="grouped2", tag="first3", align_bytes=64)
         times(grouped2[:], apart2, value_cols)
         apart3 = sb.tile([P, P, PACK], F32, name="apart3")
@@ -195,5 +196,5 @@ def tile_attend_passedthrough_apartvalues_lean_kernel(
         for h in range(2):
             times(grouped3[:, h * I // 2 : (h + 1) * I // 2], apart3[:, h * P // 2 : (h + 1) * P // 2, :], value_cols)
         codes3, scales3 = quantise("value3", grouped3[:], P)
-        finish(2, [(codes2[:], scales2[:])], "out2", nc.sync)
-        finish(3, [(codes3[:], scales3[:])], "out3", nc.scalar)
+        finish(2, [(codes2[:], scales2[:])], "score_bank0", nc.sync)
+        finish(3, [(codes3[:], scales3[:])], "score_bank1", nc.scalar)

@@ -44,7 +44,7 @@ def tile_attend_passedthrough_apartvalues_lean_kernel(
         def load_rows(name, src, b):
             tile = sb.tile([P, src.shape[1]], F32, name=name, tag=name, align_bytes=64)
             nc.sync.dma_start(tile[:], src[b * P : (b + 1) * P, :])
-            return tile
+            return tile[:]
 
         def turn(bank, columns, start, stop):
             for t in range(PACK):
@@ -75,10 +75,11 @@ def tile_attend_passedthrough_apartvalues_lean_kernel(
             key_word_pool[:].bitcast(I32), keys_words[0].rearrange("p n t -> p (n t)").bitcast(I32)
         )
         store_list = load_list("store_list", offs4)
-        second[0] = load_rows("second0", vals2, 0)
+        second_pair = sb.tile([P, 2, X], F32, name="second_pair", tag="second_pair", align_bytes=64)
+        nc.sync.dma_start(second_pair[:], vals2[: 2 * P, :].rearrange("(j p) x -> p j x", j=2))
+        second[0], second[1] = second_pair[:, 0, :], second_pair[:, 1, :]
         first[0] = load_rows("first0", vals, 0)
         put_list = load_list("put_list", offs2)
-        second[1] = load_rows("second1", vals2, 1)
         fetch_list = load_list("fetch_list", offs3)
         value_cols = load_columns("value_cols", value_factor)
         weight_cols = load_columns("weight_cols", weight_factor)
@@ -93,12 +94,12 @@ def tile_attend_passedthrough_apartvalues_lean_kernel(
         nc.gpsimd.memset(places[:], 0.0)
 
         def gather_on_scalar(picked, window, offsets, scale):
-            nc.scalar.activation(picked, window[:].indirect(offsets[:]), COPY, scale=scale)
+            nc.scalar.activation(picked, window.indirect(offsets[:]), COPY, scale=scale)
             return lambda t: picked[:, t:I:PACK]
 
         def gather_on_vector(name, window, offsets):
             dealt = sb.tile([P, PACK, P], F32, name=name)
-            nc.vector.tensor_copy(dealt[:].rearrange("p t s -> p s t"), window[:].indirect(offsets[:]))
+            nc.vector.tensor_copy(dealt[:].rearrange("p t s -> p s t"), window.indirect(offsets[:]))
             return lambda t: dealt[:, t, :]
 
         def open_block(b, picked):
@@ -158,14 +159,14 @@ def tile_attend_passedthrough_apartvalues_lean_kernel(
         banks = [open_block(0, minus_second0[:])]
         weight_bank = ps.tile([P, PACK, Q], F32, name="weight_bank")
         turn(weight_bank, lambda t: scores[:, t:I:PACK], True, False)
+        minus_second1 = sb.tile([P, I], F32, name="minus_second1")
+        banks.append(open_block(1, minus_second1[:]))
 
         first_picked0 = sb.tile([P, I], F32, name="first_picked0", tag="picked")
         turn(banks[0], gather_on_scalar(first_picked0[:], first[0], token_list, 1.0), False, True)
-        minus_second1 = sb.tile([P, I], F32, name="minus_second1")
-        banks.append(open_block(1, minus_second1[:]))
-        apart0 = absolute(0, "second1")
+        apart0 = absolute(0, "second_pair")
         fetched = sb.tile([P, I], F32, name="fetched", tag="picked")
-        turn(weight_bank, gather_on_scalar(fetched[:], places, fetch_list, 1.0), False, True)
+        turn(weight_bank, gather_on_scalar(fetched[:], places[:], fetch_list, 1.0), False, True)
 
         turn(banks[1], gather_on_vector("first_dealt1", first[1], token_list), False, True)
         minus_second2, grouped0 = over_first(1)
@@ -195,6 +196,13 @@ def tile_attend_passedthrough_apartvalues_lean_kernel(
         grouped3 = sb.tile([P, I], BF16, name="grouped3", align_bytes=64)
         for h in range(2):
             times(grouped3[:, h * I // 2 : (h + 1) * I // 2], apart3[:, h * P // 2 : (h + 1) * P // 2, :], value_cols)
-        codes3, scales3 = quantise("value3", grouped3[:], P)
+        codes3 = sb.tile([P, P], U32, name="value3_codes", align_bytes=64)
+        scales3 = sb.tile([P, P], U8, name="value3_scales", align_bytes=64)
+        for h in range(2):
+            columns = slice(h * P // 2, (h + 1) * P // 2)
+            nc.vector.quantize_mx(
+                out=codes3[:, columns].bitcast(FP8X4), scales=scales3[:, columns],
+                in_=grouped3[:, h * I // 2 : (h + 1) * I // 2],
+            )
         finish(2, [(codes2[:], scales2[:])], "score_bank0", nc.sync)
         finish(3, [(codes3[:], scales3[:])], "score_bank1", nc.scalar)

@@ -68,12 +68,12 @@ def tile_attend_passedthrough_apartvalues_lean_kernel(
         query_raw = sb.tile([P, PACK, Q], F32, name="query_raw")
         nc.sync.dma_start(query_raw[:], query.rearrange("(p t) q -> p t q", t=PACK))
         token_list = load_list("token_list", offs)
-        for f in range(PACK):
-            nc.sync.dma_start(key_scale_pool[f:P:32, :].bitcast(I32), keys_scales[0, f:16:PACK, :].bitcast(I32))
         key_word_pool = sb.tile([P, T], U32, name="key_word_pool")
         nc.sync.dma_start(
             key_word_pool[:].bitcast(I32), keys_words[0].rearrange("p n t -> p (n t)").bitcast(I32)
         )
+        for f in range(PACK):
+            nc.sync.dma_start(key_scale_pool[f:P:32, :].bitcast(I32), keys_scales[0, f:16:PACK, :].bitcast(I32))
         store_list = load_list("store_list", offs4)
         second_pair = sb.tile([P, 2, X], F32, name="second_pair", tag="second_pair", align_bytes=64)
         nc.sync.dma_start(second_pair[:], vals2[: 2 * P, :].rearrange("(j p) x -> p j x", j=2))
@@ -134,21 +134,21 @@ def tile_attend_passedthrough_apartvalues_lean_kernel(
             nc.scalar.copy(result[:], bank[:])
             queue.dma_start(out[:, b0 * P : b0 * P + width], result[:])
 
-        key_scales = sb.tile([P, I], U8, name="key_scales", align_bytes=64)
-        nc.vector.tensor_copy(key_scales[:], key_scale_pool[:].indirect(token_list[:]))
         query_grouped = sb.tile([P, Q, PACK], BF16, name="query_grouped", align_bytes=64)
         nc.scalar.copy(query_grouped[:], query_raw[:].rearrange("p t q -> p q t"))
         query_codes, query_scales = quantise("query", query_grouped[:].rearrange("p c t -> p (c t)"), Q)
         scores = sb.tile([P, I], F32, name="scores")
         half = I // 2
         key_words = [sb.tile([P, half], U32, name="key_words%d" % h, align_bytes=64) for h in range(2)]
+        key_scales = [sb.tile([P, half], U8, name="key_scales%d" % h, align_bytes=64) for h in range(2)]
         score_banks = [ps.tile([P, half], F32, name="score_bank%d" % h, tag="score_bank%d" % h) for h in range(2)]
         for h in range(2):
             entries = token_list[:, h * half // 16 : (h + 1) * half // 16]
             nc.vector.tensor_copy(key_words[h][:], key_word_pool[:].indirect(entries))
+            nc.vector.tensor_copy(key_scales[h][:], key_scale_pool[:].indirect(entries))
             nc.tensor.matmul_mx(
                 out=score_banks[h][:], lhsT=query_codes[:].bitcast(FP8X4), lhsT_scale=query_scales[:],
-                rhs=key_words[h][:].bitcast(FP8X4), rhs_scale=key_scales[:, h * half : (h + 1) * half],
+                rhs=key_words[h][:].bitcast(FP8X4), rhs_scale=key_scales[h][:],
                 start=True, stop=True,
             )
         for h in range(2):

from contextlib import ExitStack

import concourse.mybir as mybir
from concourse.masks import make_identity

D, T, I, Q, E, Z, X = 512, 2048, 512, 128, 512, 1024, 1024
FLOPS = 2 * Q * D * I + 2 * Q * I * E

F32 = mybir.dt.float32
BF16 = mybir.dt.bfloat16
I32 = mybir.dt.int32
U32 = mybir.dt.uint32
U16 = mybir.dt.uint16
U8 = mybir.dt.uint8
FP8X4 = mybir.dt.float8_e4m3fn_x4
COPY = mybir.ActivationFunctionType.Copy
ABS = mybir.ActivationFunctionType.Abs
MULT = mybir.AluOpType.mult

P = 128
PACK = 4
BLOCKS = E // P
LIST_COLS = I // 16


def tile_attend_passedthrough_apartvalues_lean_kernel(
    tc, query, keys_words, keys_scales, weight_factor, vals, vals2, value_factor, offs, offs2, offs3, offs4, out
):
    nc = tc.nc
    with ExitStack() as ctx:
        sb = ctx.enter_context(tc.tile_pool(name="sb", bufs=1))
        ps = ctx.enter_context(tc.psum_pool(name="ps", bufs=1))

        def load_list(name, src):
            tile = sb.tile([P, LIST_COLS], U16, name=name)
            nc.sync.dma_start(tile[:], src)
            return tile

        def load_columns(name, src):
            tile = sb.tile([P, PACK], F32, name=name)
            nc.sync.dma_start(tile[:], src.rearrange("o (p t) -> (o p) t", t=PACK))
            return tile

        def load_rows(name, src, b):
            tile = sb.tile([P, src.shape[1]], F32, name=name, tag=name, align_bytes=64)
            nc.sync.dma_start(tile[:], src[b * P : (b + 1) * P, :])
            return tile[:]

        def turn(bank, columns, start, stop):
            for t in range(PACK):
                nc.tensor.matmul(
                    bank[:, t, :], columns(t), identity[:], is_transpose=True,
                    start=start and t == 0, stop=stop and t == PACK - 1,
                )

        def quantise(name, grouped, width):
            codes = sb.tile([P, width], U32, name=name + "_codes", align_bytes=64)
            scales = sb.tile([P, width], U8, name=name + "_scales", align_bytes=64)
            nc.vector.quantize_mx(
                out=codes[:].bitcast(FP8X4), scales=scales[:], in_=grouped
            )
            return codes, scales

        first = [None] * BLOCKS
        second = [None] * BLOCKS
        key_scale_pool = sb.tile([P, T], U8, name="key_scale_pool")
        nc.gpsimd.memset(key_scale_pool[:].bitcast(I32), 0)
        query_raw = sb.tile([P, PACK, Q], F32, name="query_raw")
        nc.sync.dma_start(query_raw[:], query.rearrange("(p t) q -> p t q", t=PACK))
        token_list = load_list("token_list", offs)
        key_word_pool = sb.tile([P, T], U32, name="key_word_pool")
        nc.sync.dma_start(
            key_word_pool[:].bitcast(I32), keys_words[0].rearrange("p n t -> p (n t)").bitcast(I32)
        )
        for f in range(PACK):
            nc.sync.dma_start(key_scale_pool[f:P:32, :].bitcast(I32), keys_scales[0, f:16:PACK, :].bitcast(I32))
        store_list = load_list("store_list", offs4)
        second_pair = sb.tile([P, 2, X], F32, name="second_pair", tag="second_pair", align_bytes=64)
        nc.sync.dma_start(second_pair[:], vals2[: 2 * P, :].rearrange("(j p) x -> p j x", j=2))
        second[0], second[1] = second_pair[:, 0, :], second_pair[:, 1, :]
        first[0] = load_rows("first0", vals, 0)
        put_list = load_list("put_list", offs2)
        fetch_list = load_list("fetch_list", offs3)
        value_cols = load_columns("value_cols", value_factor)
        weight_cols = load_columns("weight_cols", weight_factor)
        first[1] = load_rows("first1", vals, 1)
        for b in range(2, BLOCKS):
            second[b] = load_rows("second%d" % b, vals2, b)
            first[b] = load_rows("first%d" % b, vals, b)

        identity = sb.tile([P, P], F32, name="identity")
        make_identity(nc, identity[:])
        places = sb.tile([P, Z], F32, name="places")
        nc.gpsimd.memset(places[:], 0.0)

        def gather_on_scalar(picked, window, offsets, scale):
            nc.scalar.activation(picked, window.indirect(offsets[:]), COPY, scale=scale)
            return lambda t: picked[:, t:I:PACK]

        def gather_on_vector(name, window, offsets):
            dealt = sb.tile([P, PACK, P], F32, name=name)
            nc.vector.tensor_copy(dealt[:].rearrange("p t s -> p s t"), window.indirect(offsets[:]))
            return lambda t: dealt[:, t, :]

        def open_block(b, picked):
            bank = ps.tile([P, PACK, P], F32, name="value_bank%d" % b, tag="value_bank%d" % b)
            turn(bank, gather_on_scalar(picked, second[b], store_list, -1.0), True, False)
            return bank

        def absolute(b, tag):
            apart = sb.tile([P, P, PACK], F32, name="apart%d" % b, tag=tag, align_bytes=64)
            nc.scalar.activation(apart[:], banks[b][:].rearrange("p t e -> p e t"), ABS)
            return apart[:]

        def times(grouped, values, cols):
            nc.vector.tensor_tensor(
                grouped.rearrange("p (c t) -> p c t", t=PACK), values,
                cols[:].unsqueeze(1).to_broadcast([P, values.shape[1], PACK]), MULT,
            )

        def over_first(b):
            tenant = sb.tile([P, 2 * I], F32, name="over_first%d" % b, tag="first%d" % b, align_bytes=64)
            return tenant[:, :I], tenant[:, I:].bitcast(BF16)

        def finish(b0, operands, tag, queue):
            width = len(operands) * P
            bank = ps.tile([P, width], F32, name="out_bank%d" % b0, tag=tag)
            for j, (codes, scales) in enumerate(operands):
                nc.tensor.matmul_mx(
                    out=bank[:, j * P : (j + 1) * P], lhsT=weight_codes.bitcast(FP8X4), lhsT_scale=weight_scales,
                    rhs=codes.bitcast(FP8X4), rhs_scale=scales, start=True, stop=True,
                )
            result = sb.tile([P, width], F32, name="result%d" % b0)
            nc.scalar.copy(result[:], bank[:])
            queue.dma_start(out[:, b0 * P : b0 * P + width], result[:])

        query_grouped = sb.tile([P, Q, PACK], BF16, name="query_grouped", align_bytes=64)
        nc.scalar.copy(query_grouped[:], query_raw[:].rearrange("p t q -> p q t"))
        query_codes, query_scales = quantise("query", query_grouped[:].rearrange("p c t -> p (c t)"), Q)
        scores = sb.tile([P, I], F32, name="scores")
        half = I // 2
        key_words = [sb.tile([P, half], U32, name="key_words%d" % h, align_bytes=64) for h in range(2)]
        key_scales = [sb.tile([P, half], U8, name="key_scales%d" % h, align_bytes=64) for h in range(2)]
        score_banks = [ps.tile([P, half], F32, name="score_bank%d" % h, tag="score_bank%d" % h) for h in range(2)]
        for h in range(2):
            entries = token_list[:, h * half // 16 : (h + 1) * half // 16]
            nc.vector.tensor_copy(key_words[h][:], key_word_pool[:].indirect(entries))
            nc.vector.tensor_copy(key_scales[h][:], key_scale_pool[:].indirect(entries))
            nc.tensor.matmul_mx(
                out=score_banks[h][:], lhsT=query_codes[:].bitcast(FP8X4), lhsT_scale=query_scales[:],
                rhs=key_words[h][:].bitcast(FP8X4), rhs_scale=key_scales[h][:],
                start=True, stop=True,
            )
        for h in range(2):
            nc.vector.tensor_copy(scores[:, h * half : (h + 1) * half], score_banks[h][:])
        nc.vector.tensor_copy(places[:].indirect(put_list[:]), scores[:])

        minus_second0 = sb.tile([P, I], F32, name="minus_second0")
        banks = [open_block(0, minus_second0[:])]
        weight_bank = ps.tile([P, PACK, Q], F32, name="weight_bank")
        turn(weight_bank, lambda t: scores[:, t:I:PACK], True, False)
        minus_second1 = sb.tile([P, I], F32, name="minus_second1")
        banks.append(open_block(1, minus_second1[:]))

        first_picked0 = sb.tile([P, I], F32, name="first_picked0", tag="picked")
        turn(banks[0], gather_on_scalar(first_picked0[:], first[0], token_list, 1.0), False, True)
        apart0 = absolute(0, "second_pair")
        fetched = sb.tile([P, I], F32, name="fetched", tag="picked")
        turn(weight_bank, gather_on_scalar(fetched[:], places[:], fetch_list, 1.0), False, True)

        turn(banks[1], gather_on_vector("first_dealt1", first[1], token_list), False, True)
        minus_second2, grouped0 = over_first(1)
        times(grouped0[:, :I], apart0, value_cols)
        codes0, scales0 = quantise("value0", grouped0[:, :I], P)
        banks.append(open_block(2, minus_second2))
        apart1 = absolute(1, "second2")

        turn(banks[2], gather_on_vector("first_dealt2", first[2], token_list), False, True)
        minus_second3, grouped1 = over_first(2)
        times(grouped1[:, :I], weight_bank[:].rearrange("p t q -> p q t"), weight_cols)
        times(grouped1[:, I:], apart1, value_cols)
        codes1, scales1 = quantise("value1", grouped1, Q + P)
        weight_codes, weight_scales = codes1[:, :Q], scales1[:, :Q]
        banks.append(open_block(3, minus_second3))
        apart2 = absolute(2, "second3")

        turn(banks[3], gather_on_vector("first_dealt3", first[3], token_list), False, True)
        finish(0, [(codes0[:], scales0[:]), (codes1[:, Q:], scales1[:, Q:])], "value_bank2", nc.sync)
        grouped2 = sb.tile([P, I], BF16, name="grouped2", tag="first3", align_bytes=64)
        times(grouped2[:], apart2, value_cols)
        apart3 = sb.tile([P, P, PACK], F32, name="apart3")
        for h in range(2):
            columns = slice(h * P // 2, (h + 1) * P // 2)
            nc.scalar.activation(apart3[:, columns, :], banks[3][:, :, columns].rearrange("p t e -> p e t"), ABS)
        codes2, scales2 = quantise("value2", grouped2[:], P)
        grouped3 = sb.tile([P, I], BF16, name="grouped3", align_bytes=64)
        for h in range(2):
            times(grouped3[:, h * I // 2 : (h + 1) * I // 2], apart3[:, h * P // 2 : (h + 1) * P // 2, :], value_cols)
        codes3 = sb.tile([P, P], U32, name="value3_codes", align_bytes=64)
        scales3 = sb.tile([P, P], U8, name="value3_scales", align_bytes=64)
        for h in range(2):
            columns = slice(h * P // 2, (h + 1) * P // 2)
            nc.vector.quantize_mx(
                out=codes3[:, columns].bitcast(FP8X4), scales=scales3[:, columns],
                in_=grouped3[:, h * I // 2 : (h + 1) * I // 2],
            )
        finish(2, [(codes2[:], scales2[:])], "score_bank0", nc.sync)
        finish(3, [(codes3[:], scales3[:])], "score_bank1", nc.scalar)
